import numpy as np, ml_dtypes
CORES = [24,25,26,27,28,29,30,31,224,225,226,227,228,229,230,231]
N = 16
import mx_ref
NC, G, KO, SH = 128, 4, 2, 1
C = np.float32(0.019)
BF = ml_dtypes.bfloat16
def cut(t, i, w=512):
    return t[:, w * i:w * i + w]
def tile(rs):
    return np.stack(rs, axis=2).reshape(128, -1).astype(BF)
def layer(w, X):
    out = []
    for i in range(G):
        for t in range(len(X)):
            p = mx_ref.matmul(mx_ref.quantize(cut(w, len(X) * i + t)), X[t])
            z = p if t == 0 else z + p
        out.append(z)
    return out
def act(Z):
    return [np.maximum(z, 0) * C for z in Z]
def inputs(rng, e, E):
    def f(*shape):
        v = (rng.standard_normal(shape, dtype=np.float32) * np.exp2(rng.integers(-2, 3, shape[:-1] + (1,)))).astype(BF)
        return mx_ref.spread((v.astype(np.float32) * np.exp2(rng.integers(-E, E + 1, shape[:-2] + (1, 1))).astype(np.float32)).astype(BF), rng, e)
    def packed(k):
        c = np.zeros((N, 128, k * 512), np.uint8); s = np.zeros((N, 128, k * 128), np.uint8)
        for r in range(N):
            for i in range(k):
                a, b = mx_ref.quantize(f(128, 512)); c[r][:, 512 * i:512 * i + 512] = a; s[r][:, 128 * i:128 * i + 128] = mx_ref.plane(b, rng)
        return c, s
    d = {}
    d["kc"], d["ks"] = packed(KO)
    d["x"] = f(N, 128, 4 * NC)
    d["wk"] = f(N, 128, G * 512)
    d["q"] = f(N, 128, 512)
    return d
def setup_inputs(rng):
    return inputs(rng, 0, 0)
def setup_inputs_blocks(rng):
    return inputs(rng, 4, 0)
def setup_inputs_wide(rng):
    return inputs(rng, 0, 8)
def reference(kc, ks, x, wk, q):
    new = [mx_ref.quantize(tile(act(layer(wk[r], [mx_ref.quantize(x[r])])))) for r in range(N)]
    y = np.zeros((N, 128, 128 * KO + NC), np.float32)
    for o in range(N):
        old = (np.ascontiguousarray(kc[o]), mx_ref.live(ks[o]))
        qq = mx_ref.quantize(q[o])
        y[o] = np.concatenate([mx_ref.matmul(qq, old), mx_ref.matmul(qq, new[(o - SH) % N])], axis=1)
    return {"y": y}

from concourse.mybir import dt, AluOpType, ActivationFunctionType

TILE = 512
NC = 128
KO = 256
SH = 1
BANK = 512
C = 0.019
LANES = 4

SCRATCH = {
    "xb": ("sbuf", [128, TILE], "bfloat16"),
    "wb": ("sbuf", [128, 4 * TILE], "bfloat16"),
    "qb": ("sbuf", [128, TILE], "bfloat16"),
    "h": ("sbuf", [128, TILE], "bfloat16"),
    "xc": ("sbuf", [128, NC], "float8_e4m3fn_x4"),
    "xp": ("sbuf", [128, NC], "uint8"),
    "wc": ("sbuf", [128, 4 * NC], "float8_e4m3fn_x4"),
    "wp": ("sbuf", [128, 4 * NC], "uint8"),
    "qc": ("sbuf", [128, NC], "float8_e4m3fn_x4"),
    "qp": ("sbuf", [128, NC], "uint8"),
    "oldc": ("sbuf", [128, KO], "float8_e4m3fn_x4"),
    "oldp": ("sbuf", [128, KO], "uint8"),
    "minec": ("sbuf", [128, NC], "float8_e4m3fn_x4"),
    "minep": ("sbuf", [128, NC], "uint8"),
    "newc": ("sbuf", [128, NC], "float8_e4m3fn_x4"),
    "newp": ("sbuf", [128, NC], "uint8"),
    "yo": ("sbuf", [128, KO], "float32"),
    "yn": ("sbuf", [128, NC], "float32"),
    "z": ("psum", [128, 4 * BANK], "float32"),
    "s": ("psum", [128, 2 * BANK], "float32"),
}
SEMAPHORES = ["x_in", "wa_in", "wb_in", "q_in", "k_in", "x_q", "w0_q", "w1_q", "w2_q", "w3_q", "z0", "z1", "z2", "z3",
              "act", "k_q", "q_q", "old_mm", "new_mm", "old_cp", "new_cp", "old_st", "new_st", "arrived", "sent"]


def engines(mask):
    return [e for e in range(mask.bit_length()) if (mask >> e) & 1]


def rank_program(g, core, T, topo):
    rank = T.rank_of(core)
    if rank is None:
        return
    S = T.sem
    n = len(T.cores)
    dst = T.cores[(rank + SH) % n]

    g.sync.dma_start(T.xb[:], T.x[:]).then_inc(S.x_in, 16)
    g.sync.dma_start(T.wb[:, 0:3 * TILE], T.wk[:, 0:3 * TILE]).then_inc(S.wa_in, 16)
    g.sync.dma_start(T.wb[:, 3 * TILE:4 * TILE], T.wk[:, 3 * TILE:4 * TILE]).then_inc(S.wb_in, 16)
    g.sync.wait_ge(S.new_cp, 1)
    g.sync.dma_start(T.y[:, KO:KO + NC], T.yn[:]).then_inc(S.new_st, 16)
    g.sync.wait_ge(S.new_st, 16)

    g.scalar.wait_ge(S.x_in, 16)
    g.scalar.dma_start(T.qb[:], T.q[:]).then_inc(S.q_in, 16)
    g.scalar.dma_start(T.oldc[:].bitcast(dt.uint8), T.kc[:]).then_inc(S.k_in, 16)
    g.scalar.dma_start(T.oldp[:], T.ks[:]).then_inc(S.k_in, 16)
    for b in range(3):
        g.scalar.wait_ge(S["z%d" % b], 1)
        g.scalar.activation(T.h[:, b:TILE:4], T.z[:, BANK * b:BANK * b + NC], ActivationFunctionType.Relu,
                            scale=C).then_inc(S.act, 1)
    g.scalar.wait_ge(S.old_mm, 1)
    g.scalar.activation(T.yo[:], T.s[:, 0:KO], ActivationFunctionType.Copy).then_inc(S.old_cp, 1)
    g.scalar.wait_ge(S.old_cp, 1)
    g.scalar.dma_start(T.y[:, 0:KO], T.yo[:]).then_inc(S.old_st, 16)
    g.scalar.wait_ge(S.old_st, 16)

    g.vector.wait_ge(S.x_in, 16)
    g.vector.quantize_mx(T.xc[:], T.xp[:], T.xb[:]).then_inc(S.x_q, 1)
    g.vector.wait_ge(S.wa_in, 16)
    for i in range(4):
        if i == 3:
            g.vector.wait_ge(S.wb_in, 16)
        g.vector.quantize_mx(T.wc[:, NC * i:NC * i + NC], T.wp[:, NC * i:NC * i + NC],
                             T.wb[:, TILE * i:TILE * i + TILE]).then_inc(S["w%d_q" % i], 1)
    g.vector.wait_ge(S.z3, 1)
    g.vector.tensor_scalar(T.h[:, 3:TILE:4], T.z[:, BANK * 3:BANK * 3 + NC], 0.0, C, AluOpType.max,
                           AluOpType.mult).then_inc(S.act, 1)
    g.vector.wait_ge(S.act, 4)
    g.vector.quantize_mx(T.minec[:], T.minep[:], T.h[:]).then_inc(S.k_q, 1)
    g.vector.wait_ge(S.q_in, 16)
    g.vector.quantize_mx(T.qc[:], T.qp[:], T.qb[:]).then_inc(S.q_q, 1)
    g.vector.wait_ge(S.new_mm, 1)
    g.vector.tensor_copy(T.yn[:], T.s[:, BANK:BANK + NC]).then_inc(S.new_cp, 1)

    g.tensor.wait_ge(S.x_q, 1)
    for i in range(4):
        g.tensor.wait_ge(S["w%d_q" % i], 1)
        g.tensor.matmul_mx(T.z[:, BANK * i:BANK * i + NC], T.wc[:, NC * i:NC * i + NC], T.wp[:, NC * i:NC * i + NC],
                           T.xc[:], T.xp[:], True, True).then_inc(S["z%d" % i], 1)
    g.tensor.wait_ge(S.q_q, 1)
    g.tensor.wait_ge(S.k_in, 32)
    g.tensor.matmul_mx(T.s[:, 0:KO], T.qc[:], T.qp[:], T.oldc[:], T.oldp[:], True, True).then_inc(S.old_mm, 1)
    g.tensor.wait_ge(S.arrived, 2 * LANES)
    g.tensor.matmul_mx(T.s[:, BANK:BANK + NC], T.qc[:], T.qp[:], T.newc[:], T.newp[:], True, True).then_inc(S.new_mm, 1)

    rid, pid = topo.addr(dst, core)
    free = engines(topo.mask(core, dst))
    step = len(free) // (2 * LANES)
    m_codes = sum(1 << e for e in free[0::2 * step][:LANES])
    m_plane = sum(1 << e for e in free[step::2 * step][:LANES])
    g.wait_ge(S.k_q, 1)
    g.remote_dma(T.newc[:].bitcast(dt.uint8), T.minec[:].bitcast(dt.uint8), S.arrived, S.sent, pid, rid, m_codes)
    g.remote_dma(T.newp[:], T.minep[:], S.arrived, S.sent, pid, rid, m_plane)
    g.wait_ge(S.sent, 2 * LANES)
